import numpy as np
import ml_dtypes


def mxq(x, axis, fmt="e4m3"):
    dtype, down = {"e4m3": (ml_dtypes.float8_e4m3fn, 7), "e5m2": (ml_dtypes.float8_e5m2, 14)}[fmt]
    v = np.moveaxis(np.asarray(x, np.float32).astype(ml_dtypes.bfloat16).astype(np.float64), axis, -1)
    blocks = v.reshape(v.shape[:-1] + (-1, 32))
    amax = np.abs(blocks).max(-1, keepdims=True)
    byte = np.maximum(np.where(amax > 0, np.frexp(amax)[1] - 1 + 127, 0) - down, 1)
    scale = np.exp2(byte - 127.0)
    codes = (blocks / scale).astype(np.float32).astype(dtype).astype(np.float64)
    return np.moveaxis((codes * scale).reshape(v.shape), -1, axis)


WIDE = False


def mx_kscale(k):
    if not WIDE:
        return np.ones(k)
    levels = np.array([10, -10, 5, -5, 0])
    if k % 512:
        return np.exp2(np.random.permutation(np.resize(levels, k // 32))).repeat(32)
    a = np.empty((k // 512, 16))
    for p in range(k // 512):
        a[p, :8] = np.random.permutation(np.resize(levels, 8))
        for g in range(8):
            far = levels[np.abs(levels - a[p, g]) >= 10]
            a[p, g + 8] = far[np.random.randint(len(far))]
    return np.exp2(a.ravel()).repeat(32)


def f64(x):
    return np.asarray(x).astype(np.float64)


def striped(idx):
    return np.tile(idx.reshape(-1, 16).T, (8, 1)).astype(np.uint16)


def unstriped(offs):
    return offs[:16].T.reshape(-1).astype(np.int64)


K, T, D, S, V, N = 512, 1024, 4, 1024, 256, 256


def setup_inputs():
    n = np.random.standard_normal
    s = mx_kscale(K)[:, None]
    return {
        "xT": (n((K, T)) * s).astype(np.float32),
        "w": (n((K, N)) / np.sqrt(K) / s).astype(np.float32),
        "offs": striped(np.concatenate([np.random.permutation(T)[:V] for _ in range(D)])),
    }


def reference(xT, w, offs):
    idx = unstriped(offs)
    x = np.empty((K, V))
    for l in range(D):
        r = l // 4 * (4 * K // D) + l % 4 + 4 * np.arange(K // D)
        x[r] = f64(xT)[r][:, idx[l * V:(l + 1) * V]]
    xq = mxq(x, 0, "e4m3")
    return mxq(f64(w), 0, "e4m3").T @ xq

@@ -1,0 +1,77 @@
+from contextlib import ExitStack
+
+import concourse.mybir as mybir
+
+K, T, LEVELS, V, N = 512, 1024, 4, 256, 256
+P = 128
+FLOPS = 2 * K * N * V
+
+F32 = mybir.dt.float32
+BF16 = mybir.dt.bfloat16
+U32 = mybir.dt.uint32
+U16 = mybir.dt.uint16
+U8 = mybir.dt.uint8
+FP8X4 = mybir.dt.float8_e4m3fn_x4
+
+
+def tile_picked_grid_lin_none_sub_l_kernel(tc, xT, w, offs, out):
+    nc = tc.nc
+    with ExitStack() as ctx:
+        hold = ctx.enter_context(tc.tile_pool(name="hold", bufs=1))
+        psum = ctx.enter_context(tc.psum_pool(name="psum", bufs=1))
+
+        offsets = hold.tile([P, LEVELS * V // 16], U16, name="offsets")
+        tables = [hold.tile([P, T], F32, name=f"table{l}", align_bytes=64) for l in range(LEVELS)]
+        w_raw = hold.tile([P, 4, N], F32, name="w_raw", align_bytes=64)
+        xg = hold.tile([P, V, 4], BF16, name="xg", align_bytes=64)
+        x_codes = hold.tile([P, V], U32, name="x_codes", align_bytes=64)
+        x_scales = hold.tile([P, V], U8, name="x_scales", align_bytes=64)
+        wg = [hold.tile([P, P, 4], BF16, name=f"wg{h}", align_bytes=64) for h in range(2)]
+        w_codes = [hold.tile([P, P], U32, name=f"w_codes{h}", align_bytes=64) for h in range(2)]
+        w_scales = [hold.tile([P, P], U8, name=f"w_scales{h}", align_bytes=64) for h in range(2)]
+
+        levels = xT.rearrange("(f l) t -> f l t", l=LEVELS)
+        nc.sync.dma_start(tables[0][:], levels[:, 0, :])
+        nc.sync.dma_start(offsets[:], offs)
+        for l in range(1, LEVELS):
+            nc.sync.dma_start(tables[l][:], levels[:, l, :])
+        nc.sync.dma_start(w_raw[:], w.rearrange("(p j) m -> p j m", j=4))
+
+        for l in range(LEVELS):
+            pieces = 1 if l < LEVELS - 1 else 2
+            n = V // pieces
+            for i in range(pieces):
+                c0 = (l * V + i * n) // 16
+                nc.vector.tensor_copy(xg[:, i * n : (i + 1) * n, l], tables[l][:].indirect(offsets[:, c0 : c0 + n // 16]))
+        for i in range(2):
+            v = slice(i * P, (i + 1) * P)
+            nc.vector.quantize_mx(
+                out=x_codes[:, v].bitcast(FP8X4),
+                scales=x_scales[:, v],
+                in_=xg[:, v, :].rearrange("p v j -> p (v j)"),
+            )
+        nc.vector.tensor_copy(wg[0][:], w_raw[:, :, 0:P].rearrange("p j m -> p m j"))
+        nc.scalar.copy(wg[1][:], w_raw[:, :, P:N].rearrange("p j m -> p m j"))
+        for h in range(2):
+            nc.vector.quantize_mx(
+                out=w_codes[h][:].bitcast(FP8X4),
+                scales=w_scales[h][:],
+                in_=wg[h][:].rearrange("p m j -> p (m j)"),
+            )
+        for h in range(2):
+            acc = psum.tile([P, V], F32, name=f"acc{h}")
+            nc.tensor.matmul_mx(
+                out=acc[:],
+                lhsT=w_codes[h][:].bitcast(FP8X4),
+                lhsT_scale=w_scales[h][:],
+                rhs=x_codes[:].bitcast(FP8X4),
+                rhs_scale=x_scales[:],
+                start=True,
+                stop=True,
+            )
+            res = hold.tile([P, V], F32, name=f"res{h}")
+            if h == 0:
+                nc.scalar.copy(res[:], acc[:])
+            else:
+                nc.vector.tensor_copy(res[:], acc[:])
+            nc.sync.dma_start(out[h * P : (h + 1) * P, :], res[:])

@@ -26,52 +26,74 @@ def tile_picked_grid_lin_none_sub_l_kernel(tc, xT, w, offs, out):
         xg = hold.tile([P, V, 4], BF16, name="xg", align_bytes=64)
         x_codes = hold.tile([P, V], U32, name="x_codes", align_bytes=64)
         x_scales = hold.tile([P, V], U8, name="x_scales", align_bytes=64)
-        wg = [hold.tile([P, P, 4], BF16, name=f"wg{h}", align_bytes=64) for h in range(2)]
+        wg = hold.tile([P, N, 4], BF16, name="wg", align_bytes=64)
         w_codes = [hold.tile([P, P], U32, name=f"w_codes{h}", align_bytes=64) for h in range(2)]
         w_scales = [hold.tile([P, P], U8, name=f"w_scales{h}", align_bytes=64) for h in range(2)]
 
         levels = xT.rearrange("(f l) t -> f l t", l=LEVELS)
         nc.sync.dma_start(tables[0][:], levels[:, 0, :])
         nc.sync.dma_start(offsets[:], offs)
-        for l in range(1, LEVELS):
-            nc.sync.dma_start(tables[l][:], levels[:, l, :])
+        nc.sync.dma_start(tables[1][:], levels[:, 1, :])
+        nc.sync.dma_start(tables[2][:], levels[:, 2, :])
+        nc.sync.dma_start(tables[3][:], levels[:, 3, :])
         nc.sync.dma_start(w_raw[:], w.rearrange("(p j) m -> p j m", j=4))
 
-        for l in range(LEVELS):
-            pieces = 1 if l < LEVELS - 1 else 2
+        def copy_w(engine_copy, m0, m1):
+            engine_copy(
+                wg[:, m0:m1, :].rearrange("p (c i) j -> p c j i", i=4),
+                w_raw[:, :, m0:m1].rearrange("p j (c i) -> p c j i", i=4),
+            )
+
+        def quantize_w(h):
+            nc.vector.quantize_mx(
+                out=w_codes[h][:].bitcast(FP8X4),
+                scales=w_scales[h][:],
+                in_=wg[:, h * P : (h + 1) * P, :].rearrange("p m j -> p (m j)"),
+            )
+
+        def gather(l, pieces):
             n = V // pieces
             for i in range(pieces):
                 c0 = (l * V + i * n) // 16
                 nc.vector.tensor_copy(xg[:, i * n : (i + 1) * n, l], tables[l][:].indirect(offsets[:, c0 : c0 + n // 16]))
-        for i in range(2):
+
+        def quantize_x(i):
             v = slice(i * P, (i + 1) * P)
             nc.vector.quantize_mx(
                 out=x_codes[:, v].bitcast(FP8X4),
                 scales=x_scales[:, v],
                 in_=xg[:, v, :].rearrange("p v j -> p (v j)"),
             )
-        nc.vector.tensor_copy(wg[0][:], w_raw[:, :, 0:P].rearrange("p j m -> p m j"))
-        nc.scalar.copy(wg[1][:], w_raw[:, :, P:N].rearrange("p j m -> p m j"))
-        for h in range(2):
-            nc.vector.quantize_mx(
-                out=w_codes[h][:].bitcast(FP8X4),
-                scales=w_scales[h][:],
-                in_=wg[h][:].rearrange("p m j -> p (m j)"),
-            )
-        for h in range(2):
-            acc = psum.tile([P, V], F32, name=f"acc{h}")
+
+        res = [hold.tile([P, V], F32, name=f"res{h}") for h in range(2)]
+
+        def multiply(h, i):
+            acc = psum.tile([P, P], F32, name=f"acc{h}{i}")
+            v = slice(i * P, (i + 1) * P)
             nc.tensor.matmul_mx(
                 out=acc[:],
                 lhsT=w_codes[h][:].bitcast(FP8X4),
                 lhsT_scale=w_scales[h][:],
-                rhs=x_codes[:].bitcast(FP8X4),
-                rhs_scale=x_scales[:],
+                rhs=x_codes[:, v].bitcast(FP8X4),
+                rhs_scale=x_scales[:, v],
                 start=True,
                 stop=True,
             )
-            res = hold.tile([P, V], F32, name=f"res{h}")
-            if h == 0:
-                nc.scalar.copy(res[:], acc[:])
-            else:
-                nc.vector.tensor_copy(res[:], acc[:])
-            nc.sync.dma_start(out[h * P : (h + 1) * P, :], res[:])
+            return acc
+
+        for l in range(LEVELS):
+            gather(l, 1 if l < LEVELS - 1 else 2)
+        quantize_x(0)
+        quantize_x(1)
+        copy_w(nc.vector.tensor_copy, 0, 160)
+        copy_w(nc.scalar.copy, 160, N)
+        quantize_w(0)
+        quantize_w(1)
+        accs = [multiply(0, i) for i in range(2)]
+        for i in range(2):
+            nc.scalar.copy(res[0][:, i * P : (i + 1) * P], accs[i][:])
+        nc.sync.dma_start(out[0:P, :], res[0][:])
+        accs = [multiply(1, i) for i in range(2)]
+        for i in range(2):
+            nc.vector.tensor_copy(res[1][:, i * P : (i + 1) * P], accs[i][:])
+        nc.sync.dma_start(out[P:N, :], res[1][:])

@@ -85,7 +85,8 @@ def tile_picked_grid_lin_none_sub_l_kernel(tc, xT, w, offs, out):
             gather(l, 1 if l < LEVELS - 1 else 2)
         quantize_x(0)
         quantize_x(1)
-        copy_w(nc.vector.tensor_copy, 0, 160)
+        copy_w(nc.vector.tensor_copy, 0, P)
+        copy_w(nc.vector.tensor_copy, P, 160)
         copy_w(nc.scalar.copy, 160, N)
         quantize_w(0)
         quantize_w(1)

from contextlib import ExitStack

import concourse.mybir as mybir

K, T, LEVELS, V, N = 512, 1024, 4, 256, 256
P = 128
FLOPS = 2 * K * N * V

F32 = mybir.dt.float32
BF16 = mybir.dt.bfloat16
U32 = mybir.dt.uint32
U16 = mybir.dt.uint16
U8 = mybir.dt.uint8
FP8X4 = mybir.dt.float8_e4m3fn_x4


def tile_picked_grid_lin_none_sub_l_kernel(tc, xT, w, offs, out):
    nc = tc.nc
    with ExitStack() as ctx:
        hold = ctx.enter_context(tc.tile_pool(name="hold", bufs=1))
        psum = ctx.enter_context(tc.psum_pool(name="psum", bufs=1))

        offsets = hold.tile([P, LEVELS * V // 16], U16, name="offsets")
        tables = [hold.tile([P, T], F32, name=f"table{l}", align_bytes=64) for l in range(LEVELS)]
        w_raw = hold.tile([P, 4, N], F32, name="w_raw", align_bytes=64)
        xg = hold.tile([P, V, 4], BF16, name="xg", align_bytes=64)
        x_codes = hold.tile([P, V], U32, name="x_codes", align_bytes=64)
        x_scales = hold.tile([P, V], U8, name="x_scales", align_bytes=64)
        wg = hold.tile([P, N, 4], BF16, name="wg", align_bytes=64)
        w_codes = [hold.tile([P, P], U32, name=f"w_codes{h}", align_bytes=64) for h in range(2)]
        w_scales = [hold.tile([P, P], U8, name=f"w_scales{h}", align_bytes=64) for h in range(2)]

        levels = xT.rearrange("(f l) t -> f l t", l=LEVELS)
        nc.sync.dma_start(tables[0][:], levels[:, 0, :])
        nc.sync.dma_start(offsets[:], offs)
        nc.sync.dma_start(tables[1][:], levels[:, 1, :])
        nc.sync.dma_start(tables[2][:], levels[:, 2, :])
        nc.sync.dma_start(tables[3][:], levels[:, 3, :])
        nc.sync.dma_start(w_raw[:], w.rearrange("(p j) m -> p j m", j=4))

        def copy_w(engine_copy, m0, m1):
            engine_copy(
                wg[:, m0:m1, :].rearrange("p (c i) j -> p c j i", i=4),
                w_raw[:, :, m0:m1].rearrange("p j (c i) -> p c j i", i=4),
            )

        def quantize_w(h):
            nc.vector.quantize_mx(
                out=w_codes[h][:].bitcast(FP8X4),
                scales=w_scales[h][:],
                in_=wg[:, h * P : (h + 1) * P, :].rearrange("p m j -> p (m j)"),
            )

        def gather(l, pieces):
            n = V // pieces
            for i in range(pieces):
                c0 = (l * V + i * n) // 16
                nc.vector.tensor_copy(xg[:, i * n : (i + 1) * n, l], tables[l][:].indirect(offsets[:, c0 : c0 + n // 16]))

        def quantize_x(i):
            v = slice(i * P, (i + 1) * P)
            nc.vector.quantize_mx(
                out=x_codes[:, v].bitcast(FP8X4),
                scales=x_scales[:, v],
                in_=xg[:, v, :].rearrange("p v j -> p (v j)"),
            )

        res = [hold.tile([P, V], F32, name=f"res{h}") for h in range(2)]

        def multiply(h, i):
            acc = psum.tile([P, P], F32, name=f"acc{h}{i}")
            v = slice(i * P, (i + 1) * P)
            nc.tensor.matmul_mx(
                out=acc[:],
                lhsT=w_codes[h][:].bitcast(FP8X4),
                lhsT_scale=w_scales[h][:],
                rhs=x_codes[:, v].bitcast(FP8X4),
                rhs_scale=x_scales[:, v],
                start=True,
                stop=True,
            )
            return acc

        for l in range(LEVELS):
            gather(l, 1 if l < LEVELS - 1 else 2)
        quantize_x(0)
        quantize_x(1)
        copy_w(nc.vector.tensor_copy, 0, P)
        copy_w(nc.vector.tensor_copy, P, 160)
        copy_w(nc.scalar.copy, 160, N)
        quantize_w(0)
        quantize_w(1)
        accs = [multiply(0, i) for i in range(2)]
        for i in range(2):
            nc.scalar.copy(res[0][:, i * P : (i + 1) * P], accs[i][:])
        nc.sync.dma_start(out[0:P, :], res[0][:])
        accs = [multiply(1, i) for i in range(2)]
        for i in range(2):
            nc.vector.tensor_copy(res[1][:, i * P : (i + 1) * P], accs[i][:])
        nc.sync.dma_start(out[P:N, :], res[1][:])
